import numpy as np, ml_dtypes
CORES = [65,73,81,89,97,105,113,121]
N = 8
import mx_ref
NC, G = 128, 4
C = np.float32(0.047)
BF = ml_dtypes.bfloat16
def cut(t, i, w=512):
    return t[:, w * i:w * i + w]
def tile(rs):
    return np.stack(rs, axis=2).reshape(128, -1).astype(BF)
def layer(w, X):
    out = []
    for i in range(G):
        for t in range(len(X)):
            p = mx_ref.matmul(mx_ref.quantize(cut(w, len(X) * i + t)), X[t])
            z = p if t == 0 else z + p
        out.append(z)
    return out
def setup_inputs(rng):
    def f(*shape):
        return mx_ref.flush((rng.standard_normal(shape, dtype=np.float32) * np.exp2(rng.integers(-2, 3, shape[:-1] + (1,)))).astype(BF))
    return {"x": f(N, 128, 4 * NC), "w": f(N, 128, 512), "a": f(N, 128, 4 * 512), "bb": f(N, 128, 512)}
def setup_inputs_blocks(rng):
    d = setup_inputs(rng)
    for k in ("x", "w", "bb", "a"): d[k] = mx_ref.spread(d[k], rng, 4)
    return d
def setup_inputs_wide(rng):
    d = setup_inputs(rng)
    for k in ("x", "w", "bb", "a"): d[k] = mx_ref.flush((d[k].astype(np.float32) * np.exp2(rng.integers(-6, 7, (N, 1, 1))).astype(np.float32)).astype(BF))
    return d
def setup_inputs_zeros(rng):
    d = setup_inputs(rng); v = d["x"].reshape(N, 128, -1, 4).copy()
    v[np.broadcast_to((rng.random((N, 1, v.shape[2], 1)) < 0.33), v.shape)] = 0
    d["x"] = v.reshape(d["x"].shape)
    return d
def reference(x, w, a, bb):
    X = [mx_ref.quantize(x[j]) for j in range(N)]
    T = [mx_ref.quantize(tile([z * C for z in layer(a[j], [X[j]])])) for j in range(N)]
    y = np.zeros((N, 128, N * NC), np.float32)
    for r in range(N):
        qw = mx_ref.quantize(w[r]); qb = mx_ref.quantize(bb[r])
        for j in range(N):
            y[r][:, NC * j:NC * j + NC] = mx_ref.matmul(qw, X[j]) + mx_ref.matmul(qb, T[j])
    return {"y": y}

@@ -1,0 +1,205 @@
+from concourse.bass import DstId, RemoteDMATransfer
+from concourse.mybir import dt, AluOpType, ActivationFunctionType
+
+N = 8
+NC = 128
+G = 4
+C = 0.047
+CORES_ALL = 128
+PAIRS = N // 2
+
+SCRATCH = {
+    "xb": ("sbuf", [128, 512], "bfloat16"),
+    "ab": ("sbuf", [128, 4 * 512], "bfloat16"),
+    "wb": ("sbuf", [128, 512], "bfloat16"),
+    "bbb": ("sbuf", [128, 512], "bfloat16"),
+    "tb": ("sbuf", [128, 512], "bfloat16"),
+    "xc": ("sbuf", [128, N * NC], "float8_e4m3fn_x4"),
+    "xs": ("sbuf", [128, N * NC], "uint8"),
+    "tc": ("sbuf", [128, N * NC], "float8_e4m3fn_x4"),
+    "ts": ("sbuf", [128, N * NC], "uint8"),
+    "ac": ("sbuf", [128, G * NC], "float8_e4m3fn_x4"),
+    "as": ("sbuf", [128, G * NC], "uint8"),
+    "wc": ("sbuf", [128, NC], "float8_e4m3fn_x4"),
+    "ws": ("sbuf", [128, NC], "uint8"),
+    "bc": ("sbuf", [128, NC], "float8_e4m3fn_x4"),
+    "bs": ("sbuf", [128, NC], "uint8"),
+    "yb": ("sbuf", [128, N * NC], "float32"),
+    "z": ("psum", [128, 4 * 512], "float32"),
+    "yp": ("psum", [128, 4 * 512], "float32"),
+}
+SEMAPHORES = (["lx", "lw", "lb", "qx", "qw", "qb", "qt", "hx", "ht", "ls"]
+              + ["la%d" % i for i in range(G)] + ["qa%d" % i for i in range(G)]
+              + ["z%d" % i for i in range(G)] + ["e%d" % i for i in range(G)]
+              + ["xin%d" % j for j in range(N)] + ["tin%d" % j for j in range(N)]
+              + ["yp%d" % p for p in range(PAIRS)] + ["ye%d" % p for p in range(PAIRS)]
+              + ["ys%d" % p for p in range(PAIRS)])
+
+
+def _bits(mask):
+    return bin(mask).count("1")
+
+
+def _plan(rcore, cores, topo):
+    chip = topo.chip(rcore)
+    j = cores.index(rcore)
+    ring = [cores[(j + k) % N] for k in range(1, N)]
+    same = [d for d in ring if topo.may_write(rcore, d)]
+    cross = [d for d in ring if not topo.may_write(rcore, d)]
+    cross.sort(key=lambda d: 0 if topo.mates(chip, topo.chip(d)) else 1)
+    mine = [c for c in range(CORES_ALL) if topo.chip(c) == chip and c != rcore]
+    port = [c for c in mine if all(topo.may_write(c, d) for d in cross)]
+    plain = [c for c in mine if c not in port]
+    near = [c for c in port if topo.die(c) == topo.die(rcore)]
+    far = [c for c in port if topo.die(c) != topo.die(rcore)]
+    plain.sort(key=lambda c: 0 if topo.die(c) == topo.die(rcore) else 1)
+    h = {
+        near[0]: ("codes", cross[:2], True),
+        far[0]: ("codes", cross[2:], True),
+        near[1]: ("planes", cross[:2], True),
+        far[1]: ("planes", cross[2:], True),
+        plain[0]: ("codes", same[:2], True),
+        plain[1]: ("codes", same[2:], True),
+        plain[2]: ("planes", same, False),
+    }
+    return h, same
+
+
+def _view(T, phase, kind, j):
+    s = slice(NC * j, NC * j + NC)
+    if kind == "codes":
+        return T[phase + "c"][:, s].bitcast(dt.uint8)
+    return T[phase + "s"][:, s]
+
+
+def _send(g, T, topo, core, dsts, phase, kind, j, sem):
+    mask = topo.mask(core, dsts[0])
+    for d in dsts:
+        mask &= topo.mask(core, d)
+    ids = []
+    for d in dsts:
+        rid, pid, _ = topo.addr(d)
+        ids.append(DstId(rid=rid, pnc=pid))
+    v = _view(T, phase, kind, j)
+    g.remote_dma_fused([RemoteDMATransfer(dst_ids=ids, dma_engine_mask=mask, remote_sem=sem, srcs=[v],
+                                          dsts=[_view(T, phase, kind, j) for _ in dsts])], local_sem=T.sem.ls)
+    return _bits(mask)
+
+
+def _helper(g, core, T, topo, rcore):
+    cores = list(T.cores)
+    h, _ = _plan(rcore, cores, topo)
+    if core not in h:
+        return
+    kind, dsts, both = h[core]
+    j = cores.index(rcore)
+    landed = _bits(topo.mask(rcore, core))
+    left = 0
+    g.wait_ge(T.sem.hx, landed)
+    left += _send(g, T, topo, core, dsts, "x", kind, j, T.sem["xin%d" % j])
+    if both:
+        g.wait_ge(T.sem.ht, landed)
+        left += _send(g, T, topo, core, dsts, "t", kind, j, T.sem["tin%d" % j])
+    g.wait_ge(T.sem.ls, left)
+
+
+def rank_program(g, core, T, topo):
+    rank = T.rank_of(core)
+    cores = list(T.cores)
+    if rank is None:
+        for rc in cores:
+            if topo.chip(rc) == topo.chip(core):
+                _helper(g, core, T, topo, rc)
+        return
+    S = T.sem
+    h, same = _plan(core, cores, topo)
+    codes = [c for c in h if h[c][0] == "codes"]
+    planes = [c for c in h if h[c][0] == "planes"]
+    planes_t = [c for c in planes if h[c][2]]
+    own = slice(NC * rank, NC * rank + NC)
+
+    def a_tile(i):
+        return slice(512 * i, 512 * i + 512)
+    g.sync.dma_start(T.xb[:], T.x[:]).then_inc(S.lx, 16)
+    g.scalar.dma_start(T.ab[:, a_tile(0)], T.a[:, a_tile(0)]).then_inc(S.la0, 16)
+    g.sync.dma_start(T.ab[:, a_tile(1)], T.a[:, a_tile(1)]).then_inc(S.la1, 16)
+    g.scalar.dma_start(T.ab[:, a_tile(2)], T.a[:, a_tile(2)]).then_inc(S.la2, 16)
+    g.sync.dma_start(T.ab[:, a_tile(3)], T.a[:, a_tile(3)]).then_inc(S.la3, 16)
+    g.scalar.dma_start(T.wb[:], T.w[:]).then_inc(S.lw, 16)
+    g.sync.dma_start(T.bbb[:], T.bb[:]).then_inc(S.lb, 16)
+
+    left = 0
+    g.wait_ge(S.qx, 1)
+    left += _send(g, T, topo, core, codes, "x", "codes", rank, S.hx)
+    left += _send(g, T, topo, core, planes, "x", "planes", rank, S.hx)
+    g.wait_ge(S.qt, 1)
+    left += _send(g, T, topo, core, codes, "t", "codes", rank, S.ht)
+    left += _send(g, T, topo, core, planes_t, "t", "planes", rank, S.ht)
+    left += _send(g, T, topo, core, same, "t", "planes", rank, S["tin%d" % rank])
+    g.wait_ge(S.ls, left)
+
+    order = [(rank // 2 + k) % PAIRS for k in range(PAIRS)]
+    by_vector = [order[0], order[2]]
+
+    v = g.vector
+    v.wait_ge(S.lx, 16)
+    v.quantize_mx(T.xc[:, own], T.xs[:, own], T.xb[:]).then_inc(S.qx, 1)
+    for i in range(G):
+        v.wait_ge(S["la%d" % i], 16)
+        c = slice(NC * i, NC * i + NC)
+        v.quantize_mx(T.ac[:, c], T["as"][:, c], T.ab[:, a_tile(i)]).then_inc(S["qa%d" % i], 1)
+    for b in (2, 3):
+        v.wait_ge(S["z%d" % b], 1)
+        v.tensor_scalar(T.tb[:, b:512:4], T.z[:, 512 * b:512 * b + NC], C, None, AluOpType.mult).then_inc(S["e%d" % b], 1)
+    for b in range(G):
+        v.wait_ge(S["e%d" % b], 1)
+    v.quantize_mx(T.tc[:, own], T.ts[:, own], T.tb[:]).then_inc(S.qt, 1)
+    v.wait_ge(S.lw, 16)
+    v.quantize_mx(T.wc[:], T.ws[:], T.wb[:]).then_inc(S.qw, 1)
+    v.wait_ge(S.lb, 16)
+    v.quantize_mx(T.bc[:], T.bs[:], T.bbb[:]).then_inc(S.qb, 1)
+    for p in by_vector:
+        v.wait_ge(S["yp%d" % p], 1)
+        v.tensor_copy(T.yb[:, 256 * p:256 * p + 256], T.yp[:, 512 * p:512 * p + 256]).then_inc(S["ye%d" % p], 1)
+
+    te = g.tensor
+    te.wait_ge(S.qx, 1)
+    for i in range(G):
+        c = slice(NC * i, NC * i + NC)
+        te.wait_ge(S["qa%d" % i], 1)
+        te.matmul_mx(T.z[:, 512 * i:512 * i + NC], T.ac[:, c], T["as"][:, c], T.xc[:, own], T.xs[:, own],
+                     True, True).then_inc(S["z%d" % i], 1)
+
+    def arrived(phase, p):
+        for j in (2 * p, 2 * p + 1):
+            if j != rank:
+                te.wait_ge(S["%sin%d" % (phase, j)], 2 * _bits(topo.mask(cores[j], core)))
+    te.wait_ge(S.qw, 1)
+    for p in order:
+        arrived("x", p)
+        m = slice(256 * p, 256 * p + 256)
+        te.matmul_mx(T.yp[:, 512 * p:512 * p + 256], T.wc[:], T.ws[:], T.xc[:, m], T.xs[:, m], True, False)
+    te.wait_ge(S.qt, 1)
+    te.wait_ge(S.qb, 1)
+    for p in order:
+        arrived("t", p)
+        m = slice(256 * p, 256 * p + 256)
+        te.matmul_mx(T.yp[:, 512 * p:512 * p + 256], T.bc[:], T.bs[:], T.tc[:, m], T.ts[:, m], False, True).then_inc(S["yp%d" % p], 1)
+
+    sc = g.scalar
+    for b in (0, 1):
+        sc.wait_ge(S["z%d" % b], 1)
+        sc.activation(T.tb[:, b:512:4], T.z[:, 512 * b:512 * b + NC], ActivationFunctionType.Copy, scale=C).then_inc(S["e%d" % b], 1)
+    for p in order:
+        if p in by_vector:
+            continue
+        sc.wait_ge(S["yp%d" % p], 1)
+        sc.activation(T.yb[:, 256 * p:256 * p + 256], T.yp[:, 512 * p:512 * p + 256], ActivationFunctionType.Copy).then_inc(S["ye%d" % p], 1)
+        sc.wait_ge(S["ye%d" % p], 1)
+        sc.dma_start(T.y[:, 256 * p:256 * p + 256], T.yb[:, 256 * p:256 * p + 256]).then_inc(S["ys%d" % p], 16)
+    for p in by_vector:
+        g.sync.wait_ge(S["ye%d" % p], 1)
+        g.sync.dma_start(T.y[:, 256 * p:256 * p + 256], T.yb[:, 256 * p:256 * p + 256]).then_inc(S["ys%d" % p], 16)
+    for p in order:
+        q = g.sync if p in by_vector else sc
+        q.wait_ge(S["ys%d" % p], 16)

@@ -6,7 +6,6 @@ NC = 128
 G = 4
 C = 0.047
 CORES_ALL = 128
-PAIRS = N // 2
 
 SCRATCH = {
     "xb": ("sbuf", [128, 512], "bfloat16"),
@@ -25,15 +24,13 @@ SCRATCH = {
     "bc": ("sbuf", [128, NC], "float8_e4m3fn_x4"),
     "bs": ("sbuf", [128, NC], "uint8"),
     "yb": ("sbuf", [128, N * NC], "float32"),
-    "z": ("psum", [128, 4 * 512], "float32"),
-    "yp": ("psum", [128, 4 * 512], "float32"),
+    "ps": ("psum", [128, N * 512], "float32"),
 }
-SEMAPHORES = (["lx", "lw", "lb", "qx", "qw", "qb", "qt", "hx", "ht", "ls"]
+SEMAPHORES = (["lx", "lw", "lb", "qx", "qw", "qb", "qt", "hx", "ht", "ls", "st"]
               + ["la%d" % i for i in range(G)] + ["qa%d" % i for i in range(G)]
               + ["z%d" % i for i in range(G)] + ["e%d" % i for i in range(G)]
               + ["xin%d" % j for j in range(N)] + ["tin%d" % j for j in range(N)]
-              + ["yp%d" % p for p in range(PAIRS)] + ["ye%d" % p for p in range(PAIRS)]
-              + ["ys%d" % p for p in range(PAIRS)])
+              + ["yp%d" % j for j in range(N)] + ["ye%d" % j for j in range(N)])
 
 
 def _bits(mask):
@@ -49,57 +46,50 @@ def _plan(rcore, cores, topo):
     cross.sort(key=lambda d: 0 if topo.mates(chip, topo.chip(d)) else 1)
     mine = [c for c in range(CORES_ALL) if topo.chip(c) == chip and c != rcore]
     port = [c for c in mine if all(topo.may_write(c, d) for d in cross)]
-    plain = [c for c in mine if c not in port]
     near = [c for c in port if topo.die(c) == topo.die(rcore)]
     far = [c for c in port if topo.die(c) != topo.die(rcore)]
-    plain.sort(key=lambda c: 0 if topo.die(c) == topo.die(rcore) else 1)
+    plain = [c for c in mine if c not in port and topo.die(c) != topo.die(rcore)]
     h = {
-        near[0]: ("codes", cross[:2], True),
-        far[0]: ("codes", cross[2:], True),
-        near[1]: ("planes", cross[:2], True),
-        far[1]: ("planes", cross[2:], True),
-        plain[0]: ("codes", same[:2], True),
-        plain[1]: ("codes", same[2:], True),
-        plain[2]: ("planes", same, False),
+        near[0]: ("codes", cross[:2]),
+        far[0]: ("codes", cross[2:]),
+        near[1]: ("planes", cross[:2]),
+        far[1]: ("planes", cross[2:]),
+        plain[0]: ("planes", same),
     }
-    return h, same
+    return h, same, cross
 
 
-def _view(T, phase, kind, j):
-    s = slice(NC * j, NC * j + NC)
-    if kind == "codes":
-        return T[phase + "c"][:, s].bitcast(dt.uint8)
-    return T[phase + "s"][:, s]
+def _chip_mask(rcore, c, same, topo):
+    return topo.mask(rcore, c) & ~topo.mask(rcore, same[0])
 
 
-def _send(g, T, topo, core, dsts, phase, kind, j, sem):
-    mask = topo.mask(core, dsts[0])
-    for d in dsts:
-        mask &= topo.mask(core, d)
+def _send(g, T, topo, dsts, phase, kind, j, sem, mask):
+    def view():
+        s = slice(NC * j, NC * j + NC)
+        return T[phase + "c"][:, s].bitcast(dt.uint8) if kind == "codes" else T[phase + "s"][:, s]
     ids = []
     for d in dsts:
         rid, pid, _ = topo.addr(d)
         ids.append(DstId(rid=rid, pnc=pid))
-    v = _view(T, phase, kind, j)
-    g.remote_dma_fused([RemoteDMATransfer(dst_ids=ids, dma_engine_mask=mask, remote_sem=sem, srcs=[v],
-                                          dsts=[_view(T, phase, kind, j) for _ in dsts])], local_sem=T.sem.ls)
+    g.remote_dma_fused([RemoteDMATransfer(dst_ids=ids, dma_engine_mask=mask, remote_sem=sem, srcs=[view()],
+                                          dsts=[view() for _ in dsts])], local_sem=T.sem.ls)
     return _bits(mask)
 
 
 def _helper(g, core, T, topo, rcore):
     cores = list(T.cores)
-    h, _ = _plan(rcore, cores, topo)
+    h, same, _ = _plan(rcore, cores, topo)
     if core not in h:
         return
-    kind, dsts, both = h[core]
+    kind, dsts = h[core]
     j = cores.index(rcore)
-    landed = _bits(topo.mask(rcore, core))
+    landed = _bits(_chip_mask(rcore, core, same, topo))
+    mask = topo.mask(core, dsts[0])
     left = 0
     g.wait_ge(T.sem.hx, landed)
-    left += _send(g, T, topo, core, dsts, "x", kind, j, T.sem["xin%d" % j])
-    if both:
-        g.wait_ge(T.sem.ht, landed)
-        left += _send(g, T, topo, core, dsts, "t", kind, j, T.sem["tin%d" % j])
+    left += _send(g, T, topo, dsts, "x", kind, j, T.sem["xin%d" % j], mask)
+    g.wait_ge(T.sem.ht, landed)
+    left += _send(g, T, topo, dsts, "t", kind, j, T.sem["tin%d" % j], mask)
     g.wait_ge(T.sem.ls, left)
 
 
@@ -112,45 +102,50 @@ def rank_program(g, core, T, topo):
                 _helper(g, core, T, topo, rc)
         return
     S = T.sem
-    h, same = _plan(core, cores, topo)
+    h, same, cross = _plan(core, cores, topo)
     codes = [c for c in h if h[c][0] == "codes"]
     planes = [c for c in h if h[c][0] == "planes"]
-    planes_t = [c for c in planes if h[c][2]]
     own = slice(NC * rank, NC * rank + NC)
 
     def a_tile(i):
         return slice(512 * i, 512 * i + 512)
-    g.sync.dma_start(T.xb[:], T.x[:]).then_inc(S.lx, 16)
-    g.scalar.dma_start(T.ab[:, a_tile(0)], T.a[:, a_tile(0)]).then_inc(S.la0, 16)
-    g.sync.dma_start(T.ab[:, a_tile(1)], T.a[:, a_tile(1)]).then_inc(S.la1, 16)
-    g.scalar.dma_start(T.ab[:, a_tile(2)], T.a[:, a_tile(2)]).then_inc(S.la2, 16)
-    g.sync.dma_start(T.ab[:, a_tile(3)], T.a[:, a_tile(3)]).then_inc(S.la3, 16)
-    g.scalar.dma_start(T.wb[:], T.w[:]).then_inc(S.lw, 16)
-    g.sync.dma_start(T.bbb[:], T.bb[:]).then_inc(S.lb, 16)
+    g.sync.dma_start(T.xb[0:64, :], T.x[0:64, :]).then_inc(S.lx, 16)
+    g.scalar.dma_start(T.xb[64:128, :], T.x[64:128, :]).then_inc(S.lx, 16)
+    g.sync.dma_start(T.ab[:, a_tile(0)], T.a[:, a_tile(0)]).then_inc(S.la0, 16)
+    g.scalar.dma_start(T.ab[:, a_tile(1)], T.a[:, a_tile(1)]).then_inc(S.la1, 16)
+    g.sync.dma_start(T.ab[:, a_tile(2)], T.a[:, a_tile(2)]).then_inc(S.la2, 16)
+    g.scalar.dma_start(T.ab[:, a_tile(3)], T.a[:, a_tile(3)]).then_inc(S.la3, 16)
+    g.sync.dma_start(T.wb[:], T.w[:]).then_inc(S.lw, 16)
+    g.scalar.dma_start(T.bbb[:], T.bb[:]).then_inc(S.lb, 16)
 
     left = 0
-    g.wait_ge(S.qx, 1)
-    left += _send(g, T, topo, core, codes, "x", "codes", rank, S.hx)
-    left += _send(g, T, topo, core, planes, "x", "planes", rank, S.hx)
-    g.wait_ge(S.qt, 1)
-    left += _send(g, T, topo, core, codes, "t", "codes", rank, S.ht)
-    left += _send(g, T, topo, core, planes_t, "t", "planes", rank, S.ht)
-    left += _send(g, T, topo, core, same, "t", "planes", rank, S["tin%d" % rank])
+    for phase, ready, landed in (("x", S.qx, S.hx), ("t", S.qt, S.ht)):
+        g.wait_ge(ready, 1)
+        for kind, to in (("codes", codes), ("planes", planes)):
+            left += _send(g, T, topo, to, phase, kind, rank, landed, _chip_mask(core, to[0], same, topo))
+        left += _send(g, T, topo, same, phase, "codes", rank, S["%sin%d" % (phase, rank)], topo.mask(core, same[0]))
     g.wait_ge(S.ls, left)
 
-    order = [(rank // 2 + k) % PAIRS for k in range(PAIRS)]
-    by_vector = [order[0], order[2]]
+    nearby = [c for c in cross if core in _plan(c, cores, topo)[2][:2]]
+    order = [cores.index(c) for c in [core] + nearby + same + [c for c in cross if c not in nearby]]
+    by_vector = order[0::2]
+
+    def bank(j):
+        return slice(512 * j, 512 * j + NC)
+
+    def blk(j):
+        return slice(NC * j, NC * j + NC)
+    zbank = order[:G]
 
     v = g.vector
-    v.wait_ge(S.lx, 16)
+    v.wait_ge(S.lx, 32)
     v.quantize_mx(T.xc[:, own], T.xs[:, own], T.xb[:]).then_inc(S.qx, 1)
     for i in range(G):
         v.wait_ge(S["la%d" % i], 16)
-        c = slice(NC * i, NC * i + NC)
-        v.quantize_mx(T.ac[:, c], T["as"][:, c], T.ab[:, a_tile(i)]).then_inc(S["qa%d" % i], 1)
+        v.quantize_mx(T.ac[:, blk(i)], T["as"][:, blk(i)], T.ab[:, a_tile(i)]).then_inc(S["qa%d" % i], 1)
     for b in (2, 3):
         v.wait_ge(S["z%d" % b], 1)
-        v.tensor_scalar(T.tb[:, b:512:4], T.z[:, 512 * b:512 * b + NC], C, None, AluOpType.mult).then_inc(S["e%d" % b], 1)
+        v.tensor_scalar(T.tb[:, b:512:4], T.ps[:, bank(zbank[b])], C, None, AluOpType.mult).then_inc(S["e%d" % b], 1)
     for b in range(G):
         v.wait_ge(S["e%d" % b], 1)
     v.quantize_mx(T.tc[:, own], T.ts[:, own], T.tb[:]).then_inc(S.qt, 1)
@@ -158,48 +153,40 @@ def rank_program(g, core, T, topo):
     v.quantize_mx(T.wc[:], T.ws[:], T.wb[:]).then_inc(S.qw, 1)
     v.wait_ge(S.lb, 16)
     v.quantize_mx(T.bc[:], T.bs[:], T.bbb[:]).then_inc(S.qb, 1)
-    for p in by_vector:
-        v.wait_ge(S["yp%d" % p], 1)
-        v.tensor_copy(T.yb[:, 256 * p:256 * p + 256], T.yp[:, 512 * p:512 * p + 256]).then_inc(S["ye%d" % p], 1)
+    for j in by_vector:
+        v.wait_ge(S["yp%d" % j], 1)
+        v.tensor_copy(T.yb[:, blk(j)], T.ps[:, bank(j)]).then_inc(S["ye%d" % j], 1)
 
     te = g.tensor
     te.wait_ge(S.qx, 1)
     for i in range(G):
-        c = slice(NC * i, NC * i + NC)
         te.wait_ge(S["qa%d" % i], 1)
-        te.matmul_mx(T.z[:, 512 * i:512 * i + NC], T.ac[:, c], T["as"][:, c], T.xc[:, own], T.xs[:, own],
+        te.matmul_mx(T.ps[:, bank(zbank[i])], T.ac[:, blk(i)], T["as"][:, blk(i)], T.xc[:, own], T.xs[:, own],
                      True, True).then_inc(S["z%d" % i], 1)
-
-    def arrived(phase, p):
-        for j in (2 * p, 2 * p + 1):
-            if j != rank:
-                te.wait_ge(S["%sin%d" % (phase, j)], 2 * _bits(topo.mask(cores[j], core)))
-    te.wait_ge(S.qw, 1)
-    for p in order:
-        arrived("x", p)
-        m = slice(256 * p, 256 * p + 256)
-        te.matmul_mx(T.yp[:, 512 * p:512 * p + 256], T.wc[:], T.ws[:], T.xc[:, m], T.xs[:, m], True, False)
     te.wait_ge(S.qt, 1)
+    te.wait_ge(S.qw, 1)
+
+    def arrived(phase, j):
+        if j != rank:
+            te.wait_ge(S["%sin%d" % (phase, j)], 2 * _bits(topo.mask(core, same[0])))
+    for j in order:
+        arrived("x", j)
+        te.matmul_mx(T.ps[:, bank(j)], T.wc[:], T.ws[:], T.xc[:, blk(j)], T.xs[:, blk(j)], True, False)
     te.wait_ge(S.qb, 1)
-    for p in order:
-        arrived("t", p)
-        m = slice(256 * p, 256 * p + 256)
-        te.matmul_mx(T.yp[:, 512 * p:512 * p + 256], T.bc[:], T.bs[:], T.tc[:, m], T.ts[:, m], False, True).then_inc(S["yp%d" % p], 1)
+    for j in order:
+        arrived("t", j)
+        te.matmul_mx(T.ps[:, bank(j)], T.bc[:], T.bs[:], T.tc[:, blk(j)], T.ts[:, blk(j)], False, True).then_inc(S["yp%d" % j], 1)
 
     sc = g.scalar
     for b in (0, 1):
         sc.wait_ge(S["z%d" % b], 1)
-        sc.activation(T.tb[:, b:512:4], T.z[:, 512 * b:512 * b + NC], ActivationFunctionType.Copy, scale=C).then_inc(S["e%d" % b], 1)
-    for p in order:
-        if p in by_vector:
-            continue
-        sc.wait_ge(S["yp%d" % p], 1)
-        sc.activation(T.yb[:, 256 * p:256 * p + 256], T.yp[:, 512 * p:512 * p + 256], ActivationFunctionType.Copy).then_inc(S["ye%d" % p], 1)
-        sc.wait_ge(S["ye%d" % p], 1)
-        sc.dma_start(T.y[:, 256 * p:256 * p + 256], T.yb[:, 256 * p:256 * p + 256]).then_inc(S["ys%d" % p], 16)
-    for p in by_vector:
-        g.sync.wait_ge(S["ye%d" % p], 1)
-        g.sync.dma_start(T.y[:, 256 * p:256 * p + 256], T.yb[:, 256 * p:256 * p + 256]).then_inc(S["ys%d" % p], 16)
-    for p in order:
-        q = g.sync if p in by_vector else sc
-        q.wait_ge(S["ys%d" % p], 16)
+        sc.activation(T.tb[:, b:512:4], T.ps[:, bank(zbank[b])], ActivationFunctionType.Copy, scale=C).then_inc(S["e%d" % b], 1)
+    for j in order:
+        if j not in by_vector:
+            sc.wait_ge(S["yp%d" % j], 1)
+            sc.activation(T.yb[:, blk(j)], T.ps[:, bank(j)], ActivationFunctionType.Copy).then_inc(S["ye%d" % j], 1)
+    for j in order:
+        q = sc if j == order[-1] else g.sync
+        q.wait_ge(S["ye%d" % j], 1)
+        q.dma_start(T.y[:, blk(j)], T.yb[:, blk(j)]).then_inc(S.st, 16)
+    g.sync.wait_ge(S.st, 16 * N)

from concourse.bass import DstId, RemoteDMATransfer
from concourse.mybir import dt, AluOpType, ActivationFunctionType

N = 8
NC = 128
G = 4
C = 0.047
CORES_ALL = 128

SCRATCH = {
    "xb": ("sbuf", [128, 512], "bfloat16"),
    "ab": ("sbuf", [128, 4 * 512], "bfloat16"),
    "wb": ("sbuf", [128, 512], "bfloat16"),
    "bbb": ("sbuf", [128, 512], "bfloat16"),
    "tb": ("sbuf", [128, 512], "bfloat16"),
    "xc": ("sbuf", [128, N * NC], "float8_e4m3fn_x4"),
    "xs": ("sbuf", [128, N * NC], "uint8"),
    "tc": ("sbuf", [128, N * NC], "float8_e4m3fn_x4"),
    "ts": ("sbuf", [128, N * NC], "uint8"),
    "ac": ("sbuf", [128, G * NC], "float8_e4m3fn_x4"),
    "as": ("sbuf", [128, G * NC], "uint8"),
    "wc": ("sbuf", [128, NC], "float8_e4m3fn_x4"),
    "ws": ("sbuf", [128, NC], "uint8"),
    "bc": ("sbuf", [128, NC], "float8_e4m3fn_x4"),
    "bs": ("sbuf", [128, NC], "uint8"),
    "yb": ("sbuf", [128, N * NC], "float32"),
    "ps": ("psum", [128, N * 512], "float32"),
}
SEMAPHORES = (["lx", "lw", "lb", "qx", "qw", "qb", "qt", "hx", "ht", "ls", "st"]
              + ["la%d" % i for i in range(G)] + ["qa%d" % i for i in range(G)]
              + ["z%d" % i for i in range(G)] + ["e%d" % i for i in range(G)]
              + ["xin%d" % j for j in range(N)] + ["tin%d" % j for j in range(N)]
              + ["yp%d" % j for j in range(N)] + ["ye%d" % j for j in range(N)])


def _bits(mask):
    return bin(mask).count("1")


def _plan(rcore, cores, topo):
    chip = topo.chip(rcore)
    j = cores.index(rcore)
    ring = [cores[(j + k) % N] for k in range(1, N)]
    same = [d for d in ring if topo.may_write(rcore, d)]
    cross = [d for d in ring if not topo.may_write(rcore, d)]
    cross.sort(key=lambda d: 0 if topo.mates(chip, topo.chip(d)) else 1)
    mine = [c for c in range(CORES_ALL) if topo.chip(c) == chip and c != rcore]
    port = [c for c in mine if all(topo.may_write(c, d) for d in cross)]
    near = [c for c in port if topo.die(c) == topo.die(rcore)]
    far = [c for c in port if topo.die(c) != topo.die(rcore)]
    plain = [c for c in mine if c not in port and topo.die(c) != topo.die(rcore)]
    h = {
        near[0]: ("codes", cross[:2]),
        far[0]: ("codes", cross[2:]),
        near[1]: ("planes", cross[:2]),
        far[1]: ("planes", cross[2:]),
        plain[0]: ("planes", same),
    }
    return h, same, cross


def _chip_mask(rcore, c, same, topo):
    return topo.mask(rcore, c) & ~topo.mask(rcore, same[0])


def _send(g, T, topo, dsts, phase, kind, j, sem, mask):
    def view():
        s = slice(NC * j, NC * j + NC)
        return T[phase + "c"][:, s].bitcast(dt.uint8) if kind == "codes" else T[phase + "s"][:, s]
    ids = []
    for d in dsts:
        rid, pid, _ = topo.addr(d)
        ids.append(DstId(rid=rid, pnc=pid))
    g.remote_dma_fused([RemoteDMATransfer(dst_ids=ids, dma_engine_mask=mask, remote_sem=sem, srcs=[view()],
                                          dsts=[view() for _ in dsts])], local_sem=T.sem.ls)
    return _bits(mask)


def _helper(g, core, T, topo, rcore):
    cores = list(T.cores)
    h, same, _ = _plan(rcore, cores, topo)
    if core not in h:
        return
    kind, dsts = h[core]
    j = cores.index(rcore)
    landed = _bits(_chip_mask(rcore, core, same, topo))
    mask = topo.mask(core, dsts[0])
    left = 0
    g.wait_ge(T.sem.hx, landed)
    left += _send(g, T, topo, dsts, "x", kind, j, T.sem["xin%d" % j], mask)
    g.wait_ge(T.sem.ht, landed)
    left += _send(g, T, topo, dsts, "t", kind, j, T.sem["tin%d" % j], mask)
    g.wait_ge(T.sem.ls, left)


def rank_program(g, core, T, topo):
    rank = T.rank_of(core)
    cores = list(T.cores)
    if rank is None:
        for rc in cores:
            if topo.chip(rc) == topo.chip(core):
                _helper(g, core, T, topo, rc)
        return
    S = T.sem
    h, same, cross = _plan(core, cores, topo)
    codes = [c for c in h if h[c][0] == "codes"]
    planes = [c for c in h if h[c][0] == "planes"]
    own = slice(NC * rank, NC * rank + NC)

    def a_tile(i):
        return slice(512 * i, 512 * i + 512)
    g.sync.dma_start(T.xb[0:64, :], T.x[0:64, :]).then_inc(S.lx, 16)
    g.scalar.dma_start(T.xb[64:128, :], T.x[64:128, :]).then_inc(S.lx, 16)
    g.sync.dma_start(T.ab[:, a_tile(0)], T.a[:, a_tile(0)]).then_inc(S.la0, 16)
    g.scalar.dma_start(T.ab[:, a_tile(1)], T.a[:, a_tile(1)]).then_inc(S.la1, 16)
    g.sync.dma_start(T.ab[:, a_tile(2)], T.a[:, a_tile(2)]).then_inc(S.la2, 16)
    g.scalar.dma_start(T.ab[:, a_tile(3)], T.a[:, a_tile(3)]).then_inc(S.la3, 16)
    g.sync.dma_start(T.wb[:], T.w[:]).then_inc(S.lw, 16)
    g.scalar.dma_start(T.bbb[:], T.bb[:]).then_inc(S.lb, 16)

    left = 0
    for phase, ready, landed in (("x", S.qx, S.hx), ("t", S.qt, S.ht)):
        g.wait_ge(ready, 1)
        for kind, to in (("codes", codes), ("planes", planes)):
            left += _send(g, T, topo, to, phase, kind, rank, landed, _chip_mask(core, to[0], same, topo))
        left += _send(g, T, topo, same, phase, "codes", rank, S["%sin%d" % (phase, rank)], topo.mask(core, same[0]))
    g.wait_ge(S.ls, left)

    nearby = [c for c in cross if core in _plan(c, cores, topo)[2][:2]]
    order = [cores.index(c) for c in [core] + nearby + same + [c for c in cross if c not in nearby]]
    by_vector = order[0::2]

    def bank(j):
        return slice(512 * j, 512 * j + NC)

    def blk(j):
        return slice(NC * j, NC * j + NC)
    zbank = order[:G]

    v = g.vector
    v.wait_ge(S.lx, 32)
    v.quantize_mx(T.xc[:, own], T.xs[:, own], T.xb[:]).then_inc(S.qx, 1)
    for i in range(G):
        v.wait_ge(S["la%d" % i], 16)
        v.quantize_mx(T.ac[:, blk(i)], T["as"][:, blk(i)], T.ab[:, a_tile(i)]).then_inc(S["qa%d" % i], 1)
    for b in (2, 3):
        v.wait_ge(S["z%d" % b], 1)
        v.tensor_scalar(T.tb[:, b:512:4], T.ps[:, bank(zbank[b])], C, None, AluOpType.mult).then_inc(S["e%d" % b], 1)
    for b in range(G):
        v.wait_ge(S["e%d" % b], 1)
    v.quantize_mx(T.tc[:, own], T.ts[:, own], T.tb[:]).then_inc(S.qt, 1)
    v.wait_ge(S.lw, 16)
    v.quantize_mx(T.wc[:], T.ws[:], T.wb[:]).then_inc(S.qw, 1)
    v.wait_ge(S.lb, 16)
    v.quantize_mx(T.bc[:], T.bs[:], T.bbb[:]).then_inc(S.qb, 1)
    for j in by_vector:
        v.wait_ge(S["yp%d" % j], 1)
        v.tensor_copy(T.yb[:, blk(j)], T.ps[:, bank(j)]).then_inc(S["ye%d" % j], 1)

    te = g.tensor
    te.wait_ge(S.qx, 1)
    for i in range(G):
        te.wait_ge(S["qa%d" % i], 1)
        te.matmul_mx(T.ps[:, bank(zbank[i])], T.ac[:, blk(i)], T["as"][:, blk(i)], T.xc[:, own], T.xs[:, own],
                     True, True).then_inc(S["z%d" % i], 1)
    te.wait_ge(S.qt, 1)
    te.wait_ge(S.qw, 1)

    def arrived(phase, j):
        if j != rank:
            te.wait_ge(S["%sin%d" % (phase, j)], 2 * _bits(topo.mask(core, same[0])))
    for j in order:
        arrived("x", j)
        te.matmul_mx(T.ps[:, bank(j)], T.wc[:], T.ws[:], T.xc[:, blk(j)], T.xs[:, blk(j)], True, False)
    te.wait_ge(S.qb, 1)
    for j in order:
        arrived("t", j)
        te.matmul_mx(T.ps[:, bank(j)], T.bc[:], T.bs[:], T.tc[:, blk(j)], T.ts[:, blk(j)], False, True).then_inc(S["yp%d" % j], 1)

    sc = g.scalar
    for b in (0, 1):
        sc.wait_ge(S["z%d" % b], 1)
        sc.activation(T.tb[:, b:512:4], T.ps[:, bank(zbank[b])], ActivationFunctionType.Copy, scale=C).then_inc(S["e%d" % b], 1)
    for j in order:
        if j not in by_vector:
            sc.wait_ge(S["yp%d" % j], 1)
            sc.activation(T.yb[:, blk(j)], T.ps[:, bank(j)], ActivationFunctionType.Copy).then_inc(S["ye%d" % j], 1)
    for j in order:
        q = sc if j == order[-1] else g.sync
        q.wait_ge(S["ye%d" % j], 1)
        q.dma_start(T.y[:, blk(j)], T.yb[:, blk(j)]).then_inc(S.st, 16)
    g.sync.wait_ge(S.st, 16 * N)
